import numpy as np, ml_dtypes
CORES = [24,25,26,27,28,29,30,31]
N = 8
BF = ml_dtypes.bfloat16
W, S, P, M, RO = 4096, 128, 32, 4, 5
DIST = (1, 3, 6)
ST = 16 // M
def rho(d, h):
    return (((d * (2 * h + 1)) >> 1) + 613 * h) & (W - 1)
def lay(a):
    n = a.shape[-1]; return np.ascontiguousarray(a.reshape(N, 8, S // 16, 16, n).transpose(0, 1, 3, 2, 4)).reshape(N, 128, -1)
def unlay(a, n):
    return np.ascontiguousarray(a.astype(np.int64).reshape(N, 8, 16, S // 16, n).transpose(0, 1, 3, 2, 4)).reshape(N, 8, S, n)
def records(x):
    return np.ascontiguousarray(x.astype(np.int16).transpose(0, 1, 3, 2)).reshape(N * 8 * W, 16)
def heard(rec, d, h):
    return rec[np.arange(N * 8).reshape(N, 8, 1, 1) * W + rho(d, h)]
def apart(u, v):
    return np.add.reduce(np.abs(u - v), axis=-1, dtype=np.int64)
def pack(x, d, h, th, a):
    return {"X": np.ascontiguousarray(x.reshape(N, 128, W)).astype(np.float32).astype(BF), "D": lay(d).astype(np.int32), "H": lay(h).astype(np.int32),
            "th": lay(th[..., None]).astype(np.int32), "A": lay(a[..., None]).astype(np.int32)}
def runs(rng, stay):
    new = rng.random((N, 8, S, P)) >= stay; new[..., 0] = True
    i = np.maximum.accumulate(np.where(new, np.arange(P), 0), axis=-1)
    return np.take_along_axis(rng.integers(0, 16, (N, 8, S, P)), i, -1)
def setup_inputs(rng):
    x = rng.integers(-128, 128, (N, 8, 16, W)); d = rng.integers(0, W, (N, 8, S, P))
    h = runs(rng, rng.choice(np.array([0.3, 0.6, 0.8, 0.95]), (N, 8, S, 1)))
    return pack(x, d, h, rng.integers(1000, 1900, (N, 8, S)), rng.integers(0, 64, (N, 8, S)))
def setup_inputs_spread(rng):
    x = np.floor(rng.integers(-128, 128, (N, 8, 16, W)) * np.exp2(-rng.integers(0, 7, (N, 8, 1, W)).astype(np.float64))).astype(np.int64)
    d = np.floor(W * rng.random((N, 8, S, P)) ** rng.integers(1, 5, (N, 8, S, 1))).astype(np.int64); d = np.minimum(d, W - 1)
    h = runs(rng, rng.random((N, 8, S, 1)))
    th = np.minimum(np.floor(np.exp2(12 * np.sqrt(rng.random((N, 8, S))))).astype(np.int64) - 1, 4079)
    return pack(x, d, h, th, rng.integers(0, 64, (N, 8, S)))
def setup_inputs_ends(rng):
    kind = rng.integers(0, 10, (N, 8, 1, W)); top = np.where(kind < 3, 0, np.where(kind < 6, 1, rng.integers(0, 2, (N, 8, 16, W))))
    x = np.where(top == 1, 127, -128); x = x + np.where((kind == 9) & (rng.random((N, 8, 16, W)) < 0.5), 1 - 2 * top, 0)
    end = (W - 1) * rng.integers(0, 2, (N, 8, S, P))
    d = np.where(rng.random((N, 8, S, P)) < 0.8, end, rng.integers(0, W, (N, 8, S, P)))
    h = 15 * (runs(rng, 0.8) & 1); th = 4079 * rng.integers(0, 2, (N, 8, S)); a = 63 * rng.integers(0, 2, (N, 8, S))
    six = np.arange(16); c0 = rho(0, six); c1 = rho(W - 1, six); both = np.concatenate([c0, c1])
    last = int(np.argmax(rho(np.arange(W), 15) == W - 1)); d[:, :, S - 2, P - 1] = last; h[:, :, S - 2, P - 1] = 15
    chain = [0, W - 1, 0]
    for j in range(RO): chain.append((13 * chain[-1] + 4080) & (W - 1))
    far = rho(np.array(chain)[:, None], six[None, :]).reshape(-1)
    x[N - 1, 7][:, far] = 127; x[N - 1, 7][:, W - 1] = 127
    x[N - 2, 7][:, both] = -128
    for m in (1, 2, M - 1): x[N - 2, 7][:, [c0[ST * m], c1[ST * m]]] = 127
    for l in (0, S - 1):
        for q in [(N - 1 + j) % N for j in DIST]:
            x[q, 7][:, [c0[15], c1[15]]] = -128; d[q, 7, l] = end[q, 7, l]; h[q, 7, l] = 15; th[q, 7, l] = 4079; a[q, 7, l] = 63
        d[N - 1, 7, l] = end[N - 1, 7, l]; d[N - 1, 7, l, 0] = 0; h[N - 1, 7, l] = 15; th[N - 1, 7, l] = 0; a[N - 1, 7, l] = 63
    for l in (1, S - 3):
        for q in (N - 2, N - 1): d[q, 7, l] = end[q, 7, l]; h[q, 7, l] = 15; th[q, 7, l] = 4079; a[q, 7, l] = 0
    x[0, 7][:, W - 1] = -128; x[0, 7][:, 0] = 127
    for q in (0, N - 1): d[q, 7, S - 2, :P - 1] = 0; h[q, 7, S - 2, :P - 1] = 0; th[q, 7, S - 2] = 4079; a[q, 7, S - 2] = 0
    x[N - 1, 6][:, both] = 127; x[0, 6][:, both] = -128; x[N - 1, 6, 15, c1[ST]] = 126
    for l in (0, S - 1):
        for q in (0, N - 1): d[q, 6, l] = 0; d[q, 6, l, P - 1] = W - 1; h[q, 6, l] = 15; th[q, 6, l] = 4079; a[q, 6, l] = 0
    return pack(x, d, h, th, a)
def setup_inputs_corners(rng):
    k = np.arange(P); x = rng.integers(-128, 128, (N, 8, 16, W)); x[..., 0::2] = rng.integers(-4, 5, (N, 8, 16, W // 2))
    u = rng.integers(0, 16, (N, 8, S, 1)); v = rng.integers(0, 16, (N, 8, S, 1)); c = rng.integers(0, P, (N, 8, S, 1)); e = c + rng.integers(1, P, (N, 8, S, 1)); full = np.zeros((N, 8, S, P), np.int64)
    h = np.choose(rng.integers(0, 6, (N, 8, S, 1)) + full, [u + full, np.where(k % 2 == 0, u, v) + full, (u + k) & 15, np.where(k < c, u, v) + full, np.where((k >= c) & (k < e), v, u) + full, runs(rng, 0.7)])
    first = rng.choice(np.array([0, 0, 1, P // 2, P // 2 + 1, P - 2, P - 1, P - 1, P]), (1, 8, S, 1)) + np.zeros((N, 1, 1, 1), np.int64)
    loud = np.where(k < first, 0, np.where(k == first, 1, rng.integers(0, 2, (N, 8, S, P))))
    d = rng.integers(0, W, (N, 8, S, P)); d = np.where((rho(d, h) & 1) != loud, d ^ 2, d)
    a = rng.choice(np.array([0, 1, 30, 31, 32, 62, 63]), (N, 8, S))
    s = heard(records(x), d, h); far = apart(s, s[(np.arange(N) + DIST[0]) % N])
    at = np.take_along_axis(far, np.minimum(first, P - 1), -1)[..., 0]
    exact = np.minimum(np.maximum(at - (a & 31) - rng.integers(0, 2, (N, 8, S)), 0), 4079)
    w = rng.random((N, 8, S)); th = np.where(w < 0.45, rng.integers(300, 600, (N, 8, S)), np.where(w < 0.9, exact, np.where(w < 0.95, 0, 4079)))
    return pack(x, d, h, th, a)
def setup_inputs_alike(rng):
    x = np.take_along_axis(rng.integers(0, 2, (N, 8, 16, 7)), np.broadcast_to(rng.integers(0, 7, (N, 8, 1, W)), (N, 8, 16, W)), 3); x[:, 3] = x[0:1, 3]
    d = rng.integers(0, W, (N, 8, S, P)); h = runs(rng, 0.7)
    d[:, 5] = d[:, 5, :, :1]; d[:, :, ::2] = d[0:1, :, ::2]; h[:, :, ::4] = h[0:1, :, ::4]
    return pack(x, d, h, rng.integers(0, 10, (N, 8, S)), rng.choice(np.array([0, 1, 2, 32, 33, 63]), (N, 8, S)))
def setup_inputs_crowds(rng):
    x = rng.integers(-128, 128, (N, 8, 16, W)); d = rng.integers(0, W, (N, 8, S, P)); h = runs(rng, 0.7)
    th = rng.integers(1000, 1900, (N, 8, S)); a = rng.integers(0, 64, (N, 8, S)); o = [int(g) for g in rng.permutation(8)]
    for g in (o[0], o[1], o[4], o[5]): h[:, g] = rng.integers(0, 16, (N, S, 1)); th[:, g] = 0
    for g in (o[3], o[4]):
        x[:, g] = (32 * rng.permutation(8)[:N, None] - 128 + rng.integers(0, 16, (N, 16)))[..., None]; th[:, g] = 0
    still = np.zeros((N, 8, S), bool); still[:, o[2]] = True; still[int(rng.integers(0, 2))::2, o[5]] = True
    still[:, o[6]] = True; still[np.arange(N), o[6], rng.integers(0, S, N)] = False; th[:, o[6]] = 0
    return pack(x, d, h, np.where(still, 4079, th), np.where(still, rng.choice(np.array([1, 31, 63]), (N, 8, S)), a))
def check_inputs(d):
    bad = []
    for k, lo, hi in (("X", -128, 127), ("D", 0, W - 1), ("H", 0, 15), ("th", 0, 4079), ("A", 0, 63)):
        v = np.asarray(d[k]).astype(np.float64)
        if not (np.min(v) >= lo and np.max(v) <= hi): bad.append("range of " + k)
        elif np.any(v != np.floor(v)): bad.append("whole numbers of " + k)
    return bad
def reference(X, D, H, th, A):
    rec = records(X.astype(np.float32).reshape(N, 8, 16, W))
    d = unlay(D, P); h = unlay(H, P); lim = unlay(th, 1); a = unlay(A, 1); k = np.arange(P)
    for rnd in range(RO):
        x = heard(rec, d, h); y = x[(np.arange(N) + DIST[rnd % 3]) % N]; e = apart(x, y)
        over = e > lim + (a & 31); some = np.any(over, axis=-1, keepdims=True); p = np.argmax(over, axis=-1)[..., None]
        hp = np.take_along_axis(h, p, -1); ep = np.take_along_axis(e, p, -1)
        same = h == hp; c = np.add.accumulate(np.where(same, 0, 1), axis=-1)
        run = same & (c == np.take_along_axis(c, p, -1)) & some
        old = np.add.reduce(np.where(run, e, 0), axis=-1, keepdims=True)
        hm = (hp + 1 + ST * np.arange(M) + (ep & (ST - 1))) & 15
        em = np.stack([np.add.reduce(np.where(run, apart(heard(rec, d, hm[..., m:m + 1]), y), 0), axis=-1) for m in range(M)], axis=-1)
        best = np.argmin(em, axis=-1)[..., None]
        better = some & (np.take_along_axis(em, best, -1) < old); mut = some & ~better
        h = np.where(run & better, np.take_along_axis(hm, best, -1), np.where(run & mut & (k >= p), hm[..., :1], h))
        d = np.where(mut & (k == p), (13 * d + e) & (W - 1), d)
        a = a + np.where(mut, 1, 0)
    return {"yD": lay(d).astype(np.float32), "yH": lay(h).astype(np.float32), "yA": lay(a).astype(np.float32)}

from concourse.bass import DstId, RemoteDMATransfer
from concourse.mybir import dt, AluOpType, AxisListType, ActivationFunctionType

A = AluOpType
F = ActivationFunctionType
RO = 5
DIST = (1, 3, 6)
COPIES = 7
VCOPIES = 6
MAGIC = 50331648.0
WIN = [16384, 20480, 24576, 28672]
VT = (0, 1)
ORDER = (0, 2, 1, 3)
XP = 4
XV = (3,)
VPN = 4
SPN = 4
PEADD = True

SCRATCH = {"Xw": ("sbuf", [128, 4096 * COPIES], "bfloat16"),
           "Dl": ("sbuf", [128, 256], "int32"), "Hl": ("sbuf", [128, 256], "int32"),
           "tl": ("sbuf", [128, 8], "int32"), "Al": ("sbuf", [128, 8], "int32"), "thm": ("sbuf", [128, 8], "float32")}
for _t in range(3):
    SCRATCH["x%d" % _t] = ("sbuf", [128, 4096], "bfloat16")
for _t in range(RO):
    SCRATCH["y%d" % _t] = ("sbuf", [128, 4096], "bfloat16")
for _n in ("ones", "Ib", "Bt", "Bb", "Ss", "nIb", "I16", "keep"):
    SCRATCH[_n] = ("sbuf", [128, 128], "bfloat16")
for _n in ("Ih", "Bh", "V1", "Tri"):
    SCRATCH[_n] = ("sbuf", [128, 128], "float16")
SCRATCH["I4"] = ("sbuf", [128, 384], "float16")
SCRATCH["B4"] = ("sbuf", [128, 16], "float16")
SCRATCH["B16"] = ("sbuf", [128, 4], "float16")
for _n in ("selt", "sel", "sel2", "seln"):
    SCRATCH[_n] = ("sbuf", [128, 8], "bfloat16")
SCRATCH["cst"] = ("sbuf", [128, 16], "int32")
SCRATCH["rowm"] = ("sbuf", [128, 512], "bfloat16")
SCRATCH["rowg"] = ("sbuf", [128, 128], "bfloat16")
SCRATCH["rowj"] = ("sbuf", [128, 8], "bfloat16")
SCRATCH["If"] = ("sbuf", [128, 128], "float32")
for _q in range(2):
    for _n in range(4):
        SCRATCH["d%d%d" % (_n, _q)] = ("sbuf", [128, 2048], "bfloat16")
        SCRATCH["r%d%d" % (_n, _q)] = ("sbuf", [128, 2048], "bfloat16")
    for _n, _w, _d in (("Di", 128, "int32"), ("Hh", 128, "bfloat16"), ("fl", 128, "bfloat16"),
                       ("sg", 128, "bfloat16"), ("Gs", 128, "float32"), ("ths", 128, "float32"), ("ov", 128, "float16"),
                       ("fi", 128, "float16"), ("PG", 128, "float16"), ("Pe", 128, "float16"), ("ru", 128, "float16"),
                       ("mo", 128, "float16"), ("mz", 512, "float16"), ("pr", 128, "float32"), ("ls", 384, "float32"),
                       ("lz", 512, "uint16"), ("lx", 128, "uint16"), ("PD", 128, "float32"), ("ai", 128, "int32"),
                       ("ah", 128, "float16"), ("rn", 128, "bfloat16"), ("ax", 128, "bfloat16"), ("tx", 128, "float16"),
                       ("xi", 128, "int32"), ("cf", 72, "float32"), ("ci", 128, "int32"), ("ya", 4, "float32")):
        SCRATCH["%s%d" % (_n, _q)] = ("sbuf", [128, _w], _d)
    for _n in ("pA", "pZ", "pN", "pS"):
        SCRATCH["%s%d" % (_n, _q)] = ("psum", [128, 512], "float32")

SEMAPHORES = ["sv", "ss", "sp", "sg", "out", "ldD", "ldH", "ldt", "ldA"]
SEMAPHORES += ["lx%d" % k for k in [0] + list(range(VCOPIES + 1, COPIES))] + ["loc%d" % t for t in range(RO)]
SEMAPHORES += ["ar%d%d%d" % (t, q, h) for t in range(RO) for q in range(2) for h in range(XP)]

CY = 0.83 * 1.2
GC = 1.56
HOP = 120.0
SEED = 1
NOISE = 0.0
BIAS = 7000.0
SLACK = 200.0


def schedule(ops):
    n = len(ops)
    succ = [[] for _ in range(n)]
    for i, o in enumerate(ops):
        for j in o["hard"] | o["order"]:
            succ[j].append(i)
    prio = [0.0] * n
    for i in range(n - 1, -1, -1):
        prio[i] = ops[i]["cost"] + ops[i]["lat"] + max([prio[j] + HOP for j in succ[i]], default=0.0)
    rnd = SEED
    for i in range(n):
        rnd = (rnd * 1103515245 + 12345) % 2147483648
        prio[i] += (BIAS if ops[i]["ch"] == 0 else 0.0) + NOISE * (rnd / 2147483648.0 - 0.5)
    left = [len(o["hard"] | o["order"]) for o in ops]
    ready = [0.0] * n
    avail = {}
    pend = {}
    for i in range(n):
        if left[i] == 0:
            pend.setdefault(ops[i]["q"], []).append(i)
    done = []
    while len(done) < n:
        best = None
        for q, lst in pend.items():
            if not lst:
                continue
            av = avail.get(q, 0.0)
            m = min(max(av, ready[i]) for i in lst)
            c = max((i for i in lst if max(av, ready[i]) <= m + SLACK), key=lambda i: prio[i])
            st = max(av, ready[c])
            if best is None or st < best[0]:
                best = (st, c)
        st, c = best
        o = ops[c]
        pend[o["q"]].remove(c)
        avail[o["q"]] = st + o["cost"]
        o["st"] = st
        end = st + o["cost"] + o["lat"]
        done.append(c)
        for j in succ[c]:
            hop = 0.0 if c not in ops[j]["hard"] else (60.0 if ops[j]["q"] == o["q"] else HOP)
            ready[j] = max(ready[j], (end if c in ops[j]["hard"] else st) + hop)
            left[j] -= 1
            if left[j] == 0:
                pend.setdefault(ops[j]["q"], []).append(j)
    return done


def rank_program(g, core, T, topo):
    rank = T.rank_of(core)
    if rank is None:
        return
    n_ranks = len(T.cores)
    ops = []
    lastw, readers, bankacc = {}, {}, {}
    chunk = [0]

    def op(q, cost, fn, R=(), W=(), banks=(), lat=0.0, sem=None, inc=1):
        i = len(ops)
        hard, order = set(), set()
        for k in R:
            if k in lastw:
                hard.add(lastw[k])
        for k in W:
            if k in lastw:
                hard.add(lastw[k])
            hard.update(readers.get(k, ()))
        for b in banks:
            d = bankacc.setdefault(b, {})
            for e, j in d.items():
                if e == q:
                    order.add(j)
                else:
                    hard.add(j)
            d[q] = i
        for k in R:
            readers.setdefault(k, []).append(i)
        for k in W:
            lastw[k] = i
            readers[k] = []
        hard.discard(i)
        ops.append({"q": q, "cost": cost, "fn": fn, "hard": hard, "order": order - hard, "lat": lat, "sem": sem, "inc": inc, "ch": chunk[0]})
        return i

    V, S, P = g.vector, g.scalar, g.tensor

    def cyc(n):
        return max(n, 64) * CY

    def tt(out, a, b, o, R, W, n, banks=()):
        op("V", cyc(n if banks else 2 * n), lambda: [V.tensor_tensor(out, a, b, o)], R, W, banks)

    def ts(out, a, s1, s2, o0, o1, R, W, n, banks=(), half=False):
        def f():
            if o1 is None:
                return [V.tensor_scalar(out, a, s1, None, o0)]
            return [V.tensor_scalar(out, a, s1, s2, o0, o1)]
        op("V", cyc(n / 2 if half else n), f, R, W, banks)

    def cp(out, a, R, W, n, banks=(), half=False):
        op("V", cyc(n / 2 if half else n), lambda: [V.tensor_copy(out, a)], R, W, banks)

    def act(out, a, fn, R, W, n, banks=(), scale=None):
        def f():
            if scale is None:
                return [S.activation(out, a, fn)]
            return [S.activation(out, a, fn, 0.0, scale)]
        op("S", cyc(n), f, R, W, banks)

    def mms(lst, R, W, banks):
        def f():
            return [P.matmul(o, l, r, a, b) for (o, l, r, a, b, c) in lst]
        op("P", sum(x[5] for x in lst) * 0.417 * 1.2 + 5.0 * len(lst), f, R, W, banks)

    def load(out, in_, sem, W, lat):
        op("Y", 60.0, lambda: g.sync.dma_start(out, in_), (), W, (), lat, sem, 16)

    load(T.Dl[:], T.D[:], "ldD", ["Dl"], 2000.0)
    load(T.Hl[:], T.H[:], "ldH", ["Hl"], 2000.0)
    load(T.tl[:], T.th[:], "ldt", ["tl"], 2200.0)
    load(T.Al[:], T.A[:], "ldA", ["Al"], 2200.0)
    load(T.Xw[:, 0:4096], T.X[:], "lx0", ["X0"], 6500.0)

    def fill(ap, val, W, n):
        op("V", cyc(n), lambda: [V.memset(ap, val)], (), W)

    fill(T.ones[:], 1.0, ["ones"], 64)
    fill(T.rowm[0:1, :], -2040.0, ["rowm"], 256)
    fill(T.rowg[0:1, :], 16.5, ["rowg"], 64)
    fill(T.rowj[0:1, 0:4], -1.5, ["rowj0"], 64)
    fill(T.rowj[0:1, 4:8], 0.5, ["rowj1"], 64)

    def sel(out, in_, pat, cmp, base, cm, R, W, n):
        op("G", 200.0 + 2 * n * CY, lambda: [g.affine_select(out, in_, pat, cmp, 0.0, base, cm)], R, W)

    sel(T.Ib[:], T.ones[:], [[-1, 128]], A.is_equal, 0, 1, ["ones"], ["Ib"], 128)
    sel(T.keep[:], T.ones[:], [[0, 4], [1, 32]], A.is_gt, 0, 0, ["ones"], ["keep"], 128)
    sel(T.selt[:], T.ones[:, 0:8], [[-16, 8]], A.is_ge, 0, 1, ["ones"], ["selt"], 8)
    sel(T.sel[:], T.selt[:], [[16, 8]], A.is_ge, 15, -1, ["selt"], ["sel"], 8)
    sel(T.Bt[:], T.ones[:], [[-32, 4], [0, 32]], A.is_ge, 0, 1, ["ones"], ["Bt"], 128)
    sel(T.Bb[:], T.Bt[:], [[32, 4], [0, 32]], A.is_ge, 31, -1, ["Bt"], ["Bb"], 128)
    sel(T.Ss[:], T.Bb[:], [[1, 128]], A.is_ge, -1, -1, ["Bb"], ["Ss"], 128)
    op("G", 200.0, lambda: [g.iota(T.cst[:], [[4, 4], [0, 4]], 19, 0)], (), ["cst"])

    for q in range(2):
        c0 = slice(128 * q, 128 * q + 128)
        ts(T["Di%d" % q][:], T.Dl[:, c0], 613.0, None, A.add, None, ["Dl"], ["Di%d" % q], 128)
        ts(T["Hh%d" % q][:], T.Hl[:, c0], 0.5, None, A.add, None, ["Hl"], ["Hh%d" % q], 128)

    def konst():
        ts(T.nIb[:], T.Ib[:], -1.0, None, A.mult, None, ["Ib"], ["nIb"], 128, half=True)
        ts(T.I16[:], T.Ib[:], 16.0, None, A.mult, None, ["Ib"], ["I16"], 128, half=True)
        cp(T.Ih[:], T.Ib[:], ["Ib"], ["Ih"], 128, half=True)
        cp(T.If[:], T.Ib[:], ["Ib"], ["If"], 128)
        for n in (1, 2, 3):
            ts(T.I4[:, 128 * n - 128:128 * n], T.Ib[:], 4.0 * n, None, A.mult, None, ["Ib"], ["I4%d" % n], 128, half=True)
        ts(T.sel2[:], T.sel[:], 2.0, None, A.mult, None, ["sel"], ["sel2"], 8)
        ts(T.seln[:], T.sel[:], -1.0, None, A.mult, None, ["sel"], ["seln"], 8)
        tt(T.V1[:], T.Ib[:], T.Ss[:], A.subtract, ["Ib", "Ss"], ["V1"], 128)
        tt(T.Tri[:], T.Ib[:], T.Ss[:], A.add, ["Ib", "Ss"], ["Tri"], 128)
        cp(T.Bh[:], T.Bb[:], ["Bb"], ["Bh"], 128, half=True)
        for n in range(4):
            cp(T.B4[:, 4 * n:4 * n + 4], T.Bb[:, 0:128:32], ["Bb"], ["B4%d" % n], 4)
        ts(T.B16[:], T.Bb[:, 0:128:32], 16.0, None, A.mult, None, ["Bb"], ["B16"], 4)
        ts(T.thm[:], T.tl[:], -2040.0, None, A.add, None, ["tl"], ["thm"], 8)
        for q in range(2):
            cp(T["ci%d" % q][:, 120:124], T.Al[:, 4 * q:4 * q + 4], ["Al"], ["A%d" % q], 4)
            fill(T["fl%d" % q][:, 0:1], 0.0, ["fl0%d" % q], 64)
            for b in range(4):
                ts(T["tx%d" % q][:, 32 * b:32 * b + 32], T.ones[:, 0:32], T.thm[:, 4 * q + b:4 * q + b + 1], None, A.mult, None,
                   ["ones", "thm"], ["tx%d%d" % (b, q)], 32)

    B4 = ["B40", "B41", "B42", "B43"]

    def xpart(t, q):
        K = lambda s: "%s%d" % (s, q)
        chunk[0] = q
        xb = "x%d" % (t % 3)
        tt(T[K("PD")][:], T[K("Di")][:], T[K("Hh")][:], A.mult, [K("Di"), K("Hh")], [K("PD")], 128)
        ts(T[K("xi")][:], T[K("PD")][:], -306.75, None, A.add, None, [K("PD")], [K("xi")], 128)
        ts(T[K("xi")][:], T[K("xi")][:], 4095, None, A.bitwise_and, None, [K("xi")], [K("xi")], 128)
        cp(T[K("lx")][:], T[K("xi")][:], [K("xi")], [K("lx")], 128)
        w = 2048 // XP
        u = DIST[t % 3]
        dst = T.cores[(rank - u) % n_ranks]
        rid, pid = topo.addr(dst)[:2]
        for h in range(XP):
            cs = slice(2048 * q + w * h, 2048 * q + w * h + w)
            src = T.Xw[:, 0:4096].indirect(T[K("lx")][:, (w // 16) * h:(w // 16) * (h + 1)])
            R, W = ["X0", K("lx")] + (["loc%d" % (t - 3)] if t >= 3 else []), ["%s_%d%d" % (xb, q, h)]
            if h in XV or (t == 0 and q == 0 and h % 2 == 1):
                op("V", 60.0 + w * GC * CY, lambda src=src, cs=cs: [V.tensor_copy(T[xb][:, cs], src)], R, W)
            else:
                op("S", 80.0 + w * GC * CY, lambda src=src, cs=cs: [S.activation(T[xb][:, cs], src, F.Copy)], R, W)
            ar = "ar%d%d%d" % (t, q, h)
            i = op("G", 900.0, lambda cs=cs, ar=ar: g.remote_dma(T["y%d" % t][:, cs], T[xb][:, cs], T.sem[ar], T.sem["loc%d" % t],
                                                                  pid, rid, topo.mask(core, dst)),
                   ["%s_%d%d" % (xb, q, h)], [], (), 0.0, None, 0)
            a = op("arr%s" % ar, 0.0, None, (), ["y%d_%d%d" % (t, q, h)], (), 2200.0, ar, 16)
            ops[a]["order"].add(i)

    def gpart(t, q):
        K = lambda s: "%s%d" % (s, q)
        pA, pZ, A_, Z_ = T[K("pA")], T[K("pZ")], K("pA"), K("pZ")
        mms([(pA[:, 129:256], T.Ib[:], T[K("Hh")][:, 1:128], True, False, 127),
             (pA[:, 129:256], T.nIb[:], T[K("Hh")][:, 0:127], False, True, 127)], ["Ib", "nIb", K("Hh")], [K("v")], [A_])
        ts(T[K("fl")][:, 1:128], pA[:, 129:256], 0.0, None, A.not_equal, None, [K("v")], [K("fl")], 127, [A_])
        op("V", cyc(64), lambda: [V.tensor_tensor_scan(T[K("sg")][:], T.keep[:], T[K("fl")][:], 0.0, A.mult, A.add)],
           [K("fl"), K("fl0"), "keep"], [K("sg")])
        mms([(pA[:, 384:512], T.ones[0:1, :], T.rowg[0:1, :], True, False, 128),
             (pA[:, 384:512], T[K("Hh")][:], T.Ib[:], False, False, 128),
             (pA[:, 384:512], T[K("sg")][:], T.I16[:], False, True, 128)],
            ["ones", "rowg", K("Hh"), K("sg"), "Ib", "I16"], [K("GT")], [A_])
        act(T[K("Gs")][:], pA[:, 384:512], F.Copy, [K("GT")], [K("Gs")], 128, [A_])
        ci, cf = T[K("ci")], T[K("cf")]
        ts(ci[:, 124:128], ci[:, 120:124], 31, None, A.bitwise_and, None, [K("A")], [K("a31")], 4)
        cp(cf[:, 60:64], ci[:, 124:128], [K("a31")], [K("a31f")], 4)
        for b in range(4):
            act(T[K("ax")][:, 32 * b:32 * b + 32], T.ones[:, 0:32], F.Identity, ["ones", K("a31f")], [K("ax%d" % b)], 64, (),
                cf[:, 60 + b:61 + b])
        mms([(pA[:, 256:384], T[K("tx")][:], T.Ih[:], True, False, 128),
             (pA[:, 256:384], T[K("ax")][:], T.Ib[:], False, True, 128)],
            ["Ih", "Ib"] + [K("tx%d" % b) for b in range(4)] + [K("ax%d" % b) for b in range(4)], [K("GP")], [A_])
        act(T[K("ths")][:], pA[:, 256:384], F.Copy, [K("GP")], [K("ths")], 128, [A_])
        ts(T[K("ai")][:], T[K("Di")][:], 1023, None, A.bitwise_and, None, [K("Di")], [K("ai")], 128)
        cp(T[K("ah")][:], T[K("ai")][:], [K("ai")], [K("ah")], 128)
        if not PEADD:
            mms([(pZ[:, 128 * n:128 * n + 128], T.I4[:, 128 * n - 128:128 * n], T[K("ah")][:], True, True, 128) for n in (1, 2, 3)],
                [K("ah"), "I41", "I42", "I43"], [K("C"), K("Z")], [Z_])

    def epart(t, q):
        K = lambda s: "%s%d" % (s, q)
        pA, pN, A_, N_ = T[K("pA")], T[K("pN")], K("pA"), K("pN")
        xb = T["x%d" % (t % 3)]
        yb = T["y%d" % t]
        ab = T["r2%d" % q]
        for s in range(4):
            cs = slice(2048 * q + 512 * s, 2048 * q + 512 * s + 512)
            h = s * XP // 4
            bk = K("pS") if s % 2 == 0 else N_
            ks = [K("NN")] if s % 2 else []
            mms([(T[bk][:], T.Ib[:], xb[:, cs], True, False, 512), (T[bk][:], T.nIb[:], yb[:, cs], False, True, 512)],
                ["Ib", "nIb", "x%d_%d%d" % (t % 3, q, h), "y%d_%d%d" % (t, q, h)], [K("sub" + bk)] + ks, [bk])
            act(ab[:, 512 * s:512 * s + 512], T[bk][:], F.Abs, [K("sub" + bk)], [K("r2_%d" % s)], 512, [bk])
        lst = [(pA[:, 0:128], T.ones[0:1, :], T.rowm[0:1, 0:128], True, False, 128)]
        for i in range(16):
            lst.append((pA[:, i:128:16], ab[:, i:2048:16], T.sel[:], False, i == 15, 64))
        mms(lst, ["ones", "rowm", "sel"] + [K("r2_%d" % s) for s in range(4)], [K("eT")], [A_])
        tt(T[K("ov")][:], pA[:, 0:128], T[K("ths")][:], A.is_gt, [K("eT"), K("ths")], [K("ov")], 128, [A_])
        mms([(pA[:, 128:256], T.V1[:], T[K("ov")][:], True, True, 128)], ["V1", K("ov")], [K("v")], [A_])
        ts(T[K("fi")][:], pA[:, 128:256], 0.0, None, A.max, None, [K("v")], [K("fi")], 128, [A_])
        tt(T[K("Pe")][:], pA[:, 0:128], T[K("fi")][:], A.mult, [K("eT"), K("fi")], [K("Pe")], 128, [A_])
        tt(T[K("PG")][:], pA[:, 384:512], T[K("fi")][:], A.mult, [K("GT"), K("fi")], [K("PG")], 128, [A_])
        mms([(pN[:, 436:444], T.ones[0:1, :], T.rowj[0:1, :], True, False, 64),
             (pN[:, 436:444], T[K("Pe")][:], T.B4[:, 0:8], False, False, 64),
             (pN[:, 436:444], T[K("PG")][:], T.B4[:, 0:8], False, True, 64),
             (pN[:, 400:416], T[K("Pe")][:], T.B4[:], True, True, 64),
             (pN[:, 384:400], T[K("PG")][:], T.B4[:], True, True, 64)],
            [K("Pe"), K("PG"), "ones", "rowj0", "rowj1"] + B4, [K("CE"), K("NN")], [N_])
        ci, cf = T[K("ci")], T[K("cf")]
        ts(cf[:, 68:72], pN[:, 436:440], MAGIC, -MAGIC, A.add, A.add, [K("CE")], [K("rr")], 4, [N_])
        tt(cf[:, 48:52], pN[:, 440:444], cf[:, 68:72], A.subtract, [K("CE"), K("rr")], [K("jf")], 4, [N_])
        pZ, Z_ = T[K("pZ")], K("pZ")
        prk = [K("pr%d" % b) for b in range(4)]
        for b in range(4):
            bs = slice(32 * b, 32 * b + 32)
            ts(T[K("pr")][:, bs], T[K("Di")][:, bs], cf[:, 48 + b:49 + b], -306.75, A.mult, A.add, [K("Di"), K("jf")], [prk[b]], 32)
        for n in ORDER:
            ns = slice(128 * n, 128 * n + 128)
            if n == 0:
                cp(T[K("lz")][:, ns], T[K("pr")][:], prk, [K("lz0")], 128)
            elif PEADD:
                mms([(pZ[:, ns], T.I4[:, 128 * n - 128:128 * n], T[K("ah")][:], True, False, 128),
                     (pZ[:, ns], T.If[:], T[K("pr")][:], False, True, 512)], [K("ah"), "If", "I41", "I42", "I43"] + prk, [K("C%d" % n), K("Z")], [Z_])
                cp(T[K("lz")][:, ns], pZ[:, ns], [K("C%d" % n)], [K("lz%d" % n)], 128, [Z_])
            else:
                l = T[K("ls")][:, 128 * n - 128:128 * n]
                tt(l, pZ[:, ns], T[K("pr")][:], A.add, [K("C")] + prk, [K("ls%d" % n)], 128, [Z_])
                cp(T[K("lz")][:, ns], l, [K("ls%d" % n)], [K("lz%d" % n)], 128)
        cp(ci[:, 0:16], pN[:, 400:416], [K("CE")], [K("i1")], 16, [N_])
        ts(ci[:, 16:32], ci[:, 0:16], 3, None, A.bitwise_and, None, [K("i1")], [K("i2")], 16)
        tt(ci[:, 32:48], pN[:, 384:400], ci[:, 16:32], A.add, [K("CE"), K("i2")], [K("t3")], 16, [N_])
        mms([(pA[:, 256:384], T.Bh[:], T[K("PG")][:], True, True, 128)], ["Bh", K("PG")], [K("GP")], [A_])
        tt(T[K("ru")][:], pA[:, 256:384], T[K("Gs")][:], A.is_equal, [K("GP"), K("Gs")], [K("ru")], 128, [A_])
        tt(T[K("mo")][:], pA[:, 0:128], T[K("ru")][:], A.mult, [K("eT"), K("ru")], [K("mo")], 128, [A_])
        mms([(pN[:, 256:384], T[K("fi")][:], T.Ih[:], True, True, 128),
             (pN[:, 128:256], T[K("fi")][:], T.Tri[:], True, True, 128),
             (pN[:, 0:128], T[K("ru")][:], T.Ih[:], True, True, 128),
             (pN[:, 432:436], T[K("mo")][:], T.B16[:], True, True, 64)],
            ["Ih", "Tri", "B16", K("fi"), K("ru"), K("mo"), K("NN")], [K("FI"), K("FN"), K("RN"), K("OC")], [N_])
        act(T[K("rn")][:], pN[:, 0:128], F.Copy, [K("RN")], [K("rn")], 128, [N_])
        tt(ci[:, 48:64], T.cst[:], ci[:, 32:48], A.subtract, ["cst", K("t3")], [K("t2")], 16)
        ts(ci[:, 64:80], ci[:, 48:64], 12, None, A.bitwise_and, None, [K("t2")], [K("tb")], 16)
        ts(ci[:, 84:88], pN[:, 384:388], -1.0, None, A.add, None, [K("CE")], [K("gi")], 4, [N_])
        ts(ci[:, 88:92], ci[:, 84:88], 15, None, A.bitwise_and, None, [K("gi")], [K("hp")], 4)
        ts(cf[:, 12:16], pN[:, 384:388], 0.5, None, A.is_gt, None, [K("CE")], [K("sm")], 4, [N_])
        tt(T[K("PD")][:], pN[:, 256:384], T[K("Di")][:], A.mult, [K("FI"), K("Di")], [K("PD")], 128, [N_])
        op("V", cyc(128), lambda: [V.tensor_tensor_scan(T[K("pr")][:], T.keep[:], T[K("PD")][:], 0.0, A.mult, A.add)],
           [K("PD"), "keep"], prk)
        ts(cf[:, 0:4], T[K("pr")][:, 31:128:32], -613.0, None, A.add, None, prk, [K("dp")], 4)
        ts(cf[:, 4:8], cf[:, 0:4], 13.0, 2040.0, A.mult, A.add, [K("dp")], [K("nd")], 4)
        tt(ci[:, 92:96], pN[:, 400:404], cf[:, 4:8], A.add, [K("CE"), K("nd")], [K("nd2")], 4, [N_])
        ts(ci[:, 96:100], ci[:, 92:96], 4095, None, A.bitwise_and, None, [K("nd2")], [K("nd3")], 4)
        tt(cf[:, 8:12], ci[:, 96:100], cf[:, 0:4], A.subtract, [K("nd3"), K("dp")], [K("dd")], 4)

    def zpart(t, q):
        K = lambda s: "%s%d" % (s, q)
        pZ, Z_ = T[K("pZ")], K("pZ")
        yb = T["y%d" % t]
        yk = ["y%d_%d%d" % (t, q, h) for h in range(XP)]
        mms([(pZ[:], T.ones[0:1, :], T.rowm[0:1, :], True, False, 512)], ["ones", "rowm"], [K("Z"), K("C"), K("C1"), K("C2"), K("C3")], [Z_])
        for n in ORDER:
            win = T.Xw[:, 0:WIN[n]]
            wk = ["X%d" % k for k in range(WIN[n] // 4096)]
            d, r = T["d%d%d" % (n, q)], T["r%d%d" % (n, q)]
            pn = VPN if n in VT else SPN
            w = 2048 // pn
            for h in range(pn):
                cs = slice(w * h, w * h + w)
                ys = slice(2048 * q + w * h, 2048 * q + w * h + w)
                src = win.indirect(T[K("lz")][:, 128 * n + (w // 16) * h:128 * n + (w // 16) * (h + 1)])
                if n in VT:
                    op("V", 60.0 + w * GC * CY, lambda cs=cs, ys=ys, src=src, d=d: [V.tensor_tensor(d[:, cs], src, yb[:, ys], A.subtract)],
                       wk + yk + [K("lz%d" % n)], [K("d%d_%d" % (n, h))])
                    ts(r[:, cs], d[:, cs], 0.0, None, A.max, None, [K("d%d_%d" % (n, h))], [K("r%d_%d" % (n, h))], w, half=True)
                else:
                    op("S", 80.0 + w * GC * CY, lambda cs=cs, src=src, d=d: [S.activation(d[:, cs], src, F.Copy)],
                       wk + [K("lz%d" % n)], [K("d%d_%d" % (n, h))])
                    for s in range(4 * h // SPN, 4 * (h + 1) // SPN):
                        c5 = slice(512 * s, 512 * s + 512)
                        y5 = slice(2048 * q + 512 * s, 2048 * q + 512 * s + 512)
                        mms([(T[K("pS")][:], T.Ib[:], d[:, c5], True, False, 512), (T[K("pS")][:], T.nIb[:], yb[:, y5], False, True, 512)],
                            ["Ib", "nIb", K("d%d_%d" % (n, h))] + yk, [K("subpS%d" % q)], [K("pS")])
                        act(r[:, c5], T[K("pS")][:], F.Abs, [K("subpS%d" % q)], [K("r%d_%d" % (n, s))], 512, [K("pS")])
            lst = []
            last = n == ORDER[3]
            for i in range(16):
                o = pZ[:, 128 * n + i:128 * n + 128:16]
                if n in VT:
                    lst.append((o, r[:, i:2048:16], T.sel2[:], False, False, 64))
                    lst.append((o, d[:, i:2048:16], T.seln[:], False, last and i == 15, 64))
                else:
                    lst.append((o, r[:, i:2048:16], T.sel[:], False, last and i == 15, 64))
            mms(lst, ["sel", "sel2", "seln", K("Z")] + [K("r%d_%d" % (n, s)) for s in range(VPN if n in VT else 4)]
                + [K("d%d_%d" % (n, s)) for s in range(pn)], [K("Zt%d" % n)], [Z_])

    def fin(t, q):
        K = lambda s: "%s%d" % (s, q)
        pZ, Z_, pN, N_ = T[K("pZ")], K("pZ"), T[K("pN")], K("pN")
        ci, cf = T[K("ci")], T[K("cf")]
        for n in range(4):
            ns = slice(128 * n, 128 * n + 128)
            tt(T[K("mz")][:, ns], pZ[:, ns], T[K("ru")][:], A.mult, [K("Z"), K("Zt0"), K("Zt1"), K("Zt2"), K("Zt3"), K("ru")],
               [K("mz%d" % n)], 128, [Z_])
        mms([(pN[:, 416 + 4 * n:420 + 4 * n], T[K("mz")][:, 128 * n:128 * n + 128], T.B16[:], True, True, 64) for n in range(4)],
            ["B16", K("NN")] + [K("mz%d" % n) for n in range(4)], [K("EC")], [N_])
        tt(cf[:, 16:32], pN[:, 416:432], ci[:, 64:80], A.add, [K("EC"), K("tb")], [K("key")], 16, [N_])
        tt(cf[:, 32:40], cf[:, 16:24], cf[:, 24:32], A.min, [K("key")], [K("k1")], 8)
        tt(ci[:, 100:104], cf[:, 32:36], cf[:, 36:40], A.min, [K("k1")], [K("k2")], 4)
        tt(cf[:, 40:44], pN[:, 432:436], ci[:, 100:104], A.is_gt, [K("k2"), K("OC")], [K("bt")], 4, [N_])
        ts(ci[:, 104:108], ci[:, 100:104], 12, None, A.bitwise_and, None, [K("k2")], [K("m4")], 4)
        tt(ci[:, 108:112], ci[:, 104:108], cf[:, 40:44], A.mult, [K("m4"), K("bt")], [K("me")], 4)
        tt(ci[:, 112:116], ci[:, 108:112], ci[:, 32:36], A.add, [K("me"), K("t3")], [K("hr")], 4)
        ts(ci[:, 116:120], ci[:, 112:116], 15, None, A.bitwise_and, None, [K("hr")], [K("hn")], 4)
        tt(cf[:, 52:56], ci[:, 116:120], ci[:, 88:92], A.subtract, [K("hn"), K("hp")], [K("df")], 4)
        fnk = [K("fn%d" % b) for b in range(4)]
        for b in range(4):
            ps = pN[:, 128 + 32 * b:160 + 32 * b]
            ts(ps, ps, cf[:, 40 + b:41 + b], cf[:, 52 + b:53 + b], A.max, A.mult, [K("FN"), K("bt"), K("df")], [fnk[b]], 32, [N_])
        tt(pN[:, 128:256], pN[:, 128:256], T[K("rn")][:], A.mult, fnk + [K("rn")], [K("FN")] + fnk, 128, [N_])
        tt(T[K("Hh")][:], pN[:, 128:256], T[K("Hh")][:], A.add, [K("FN"), K("Hh")], [K("Hh")], 128, [N_])
        ts(cf[:, 44:48], cf[:, 40:44], -1.0, 1.0, A.mult, A.add, [K("bt")], [K("nb")], 4)
        tt(cf[:, 56:60], cf[:, 8:12], cf[:, 44:48], A.mult, [K("dd"), K("nb")], [K("md")], 4)
        fik = [K("fi%d" % b) for b in range(4)]
        for b in range(4):
            ps = pN[:, 256 + 32 * b:288 + 32 * b]
            ts(ps, ps, cf[:, 56 + b:57 + b], None, A.mult, None, [K("FI"), K("md")], [fik[b]], 32, [N_])
        tt(T[K("Di")][:], pN[:, 256:384], T[K("Di")][:], A.add, fik + [K("Di")], [K("Di"), K("FI")], 128, [N_])
        tt(cf[:, 64:68], cf[:, 12:16], cf[:, 44:48], A.mult, [K("sm"), K("nb")], [K("as")], 4)
        tt(ci[:, 120:124], ci[:, 120:124], cf[:, 64:68], A.add, [K("A"), K("as")], [K("A")], 4)

    for q in range(2):
        xpart(0, q)
    konst()
    chunk[0] = 0
    for k in range(VCOPIES + 1, COPIES):
        op("Y", 60.0, lambda k=k: g.sync.dma_start(T.Xw[:, 4096 * k:4096 * k + 4096], T.Xw[:, 0:4096]),
           ["X0"] + ["x0_0%d" % h for h in range(XP)], ["X%d" % k], (), 2000.0 + 4000.0 * (k - VCOPIES), "lx%d" % k, 16)
    for k in range(1, VCOPIES + 1):
        cp(T.Xw[:, 4096 * k:4096 * k + 4096], T.Xw[:, 0:4096], ["X0"], ["X%d" % k], 4096, half=True)
    for t in range(RO):
        for q in range(2):
            chunk[0] = q
            if t:
                xpart(t, q)
            gpart(t, q)
            epart(t, q)
            zpart(t, q)
            fin(t, q)
            if t < RO - 1:
                if q == 1:
                    op("loc%d" % t, 0.0, None, (), ["loc%d" % t], (), 1000.0, "loc%d" % t, 16 * 2 * XP)
    for q in range(2):
        K = lambda s: "%s%d" % (s, q)
        for nm, src, add, y, n in (("PD", T["Di%d" % q][:], -613.0, T.yD, 128), ("Gs", T["Hh%d" % q][:], -0.5, T.yH, 128),
                                   ("ya", T["ci%d" % q][:, 120:124], 0.0, T.yA, 4)):
            k = {"PD": "Di", "Gs": "Hh", "ya": "A"}[nm]
            ts(T[K(nm)][:], src, add, None, A.add, None, [K(k)], [K(nm)], n)
            op("Y", 60.0, lambda nm=nm, y=y, n=n, q=q: g.sync.dma_start(y[:, n * q:n * q + n], T[K2(nm, q)][:]), [K(nm)], [], (), 2000.0, "out", 16)

    seq = schedule(ops)
    SEM = {"V": "sv", "S": "ss", "P": "sp", "G": "sg"}
    ENG = {"V": g.vector, "S": g.scalar, "P": g.tensor, "G": g, "Y": g.sync}
    count = {"sv": 0, "ss": 0, "sp": 0, "sg": 0, "out": 0}
    val = {}
    clock = {q: {} for q in ENG}
    tail = {q: {} for q in ENG}
    fin_clock = {}
    for i in seq:
        o = ops[i]
        q = o["q"]
        if q not in ENG:
            val[i] = (o["sem"], o["inc"])
            fin_clock[i] = {o["sem"]: o["inc"]}
            continue
        cur = clock[q]
        need = {}
        for j in o["hard"]:
            if j in val:
                s, v = val[j]
                if cur.get(s, 0) < v and need.get(s, (0, 0))[0] < v:
                    need[s] = (v, j)
        for s in sorted(need, key=lambda s: -need[s][1]):
            v, j = need[s]
            if cur.get(s, 0) < v:
                ENG[q].wait_ge(T.sem[s], v)
                for a, b in fin_clock[j].items():
                    if cur.get(a, 0) < b:
                        cur[a] = b
        r = o["fn"]()
        if o["sem"]:
            r.then_inc(T.sem[o["sem"]], 16)
            count[o["sem"]] = count.get(o["sem"], 0) + 16
            val[i] = (o["sem"], count[o["sem"]])
            fin_clock[i] = dict(cur)
            fin_clock[i][o["sem"]] = count[o["sem"]]
        elif o["inc"]:
            s = SEM[q]
            for x in r:
                x.then_inc(T.sem[s], 1)
            count[s] += len(r)
            val[i] = (s, count[s])
            d = tail[q]
            for a, b in cur.items():
                if d.get(a, 0) < b:
                    d[a] = b
            d[s] = count[s]
            fin_clock[i] = dict(d)
    g.sync.wait_ge(T.sem.out, count["out"])
    for s in ("sv", "ss", "sp", "sg"):
        g.wait_ge(T.sem[s], count[s])
    for t in range(RO):
        g.wait_ge(T.sem["loc%d" % t], 16 * 2 * XP)


def K2(s, q):
    return "%s%d" % (s, q)
